import numpy as np
import ml_dtypes


def mxq(x, axis, fmt="e4m3"):
    dtype, down = {"e4m3": (ml_dtypes.float8_e4m3fn, 7), "e5m2": (ml_dtypes.float8_e5m2, 14)}[fmt]
    v = np.moveaxis(np.asarray(x, np.float32).astype(ml_dtypes.bfloat16).astype(np.float64), axis, -1)
    blocks = v.reshape(v.shape[:-1] + (-1, 32))
    amax = np.abs(blocks).max(-1, keepdims=True)
    byte = np.maximum(np.where(amax > 0, np.frexp(amax)[1] - 1 + 127, 0) - down, 1)
    scale = np.exp2(byte - 127.0)
    codes = (blocks / scale).astype(np.float32).astype(dtype).astype(np.float64)
    return np.moveaxis((codes * scale).reshape(v.shape), -1, axis)


WIDE = False


def mx_kscale(k):
    if not WIDE:
        return np.ones(k)
    levels = np.array([10, -10, 5, -5, 0])
    if k % 512:
        return np.exp2(np.random.permutation(np.resize(levels, k // 32))).repeat(32)
    a = np.empty((k // 512, 16))
    for p in range(k // 512):
        a[p, :8] = np.random.permutation(np.resize(levels, 8))
        for g in range(8):
            far = levels[np.abs(levels - a[p, g]) >= 10]
            a[p, g + 8] = far[np.random.randint(len(far))]
    return np.exp2(a.ravel()).repeat(32)


def f64(x):
    return np.asarray(x).astype(np.float64)


def striped(idx):
    return np.tile(idx.reshape(-1, 16).T, (8, 1)).astype(np.uint16)


def unstriped(offs):
    return offs[:16].T.reshape(-1).astype(np.int64)


K, T, E, C, N = 1536, 512, 4, 256, 256


def by_expert(wq, xq):
    return np.concatenate([wq[e].T @ xq[:, e * C:(e + 1) * C] for e in range(E)], axis=1)


def setup_inputs():
    n = np.random.standard_normal
    s = mx_kscale(K)[:, None]
    first = np.random.permutation(np.repeat(np.arange(E), T // E))
    second = (first + 1 + np.random.permutation(np.repeat(np.arange(E - 1), -(-T // (E - 1)))[:T])) % E
    while np.bincount(second, minlength=E).max() != T // E:
        load = np.bincount(second, minlength=E); hi, lo = int(load.argmax()), int(load.argmin())
        t = np.flatnonzero((second == hi) & (first != lo))[0]; second[t] = lo
    slot_token = np.empty(E * C, np.int64); pos = np.empty((2, T), np.int64); fill = np.zeros(E, np.int64)
    place = np.stack([np.random.permutation(C) for _ in range(E)])
    for r, deal in enumerate((first, second)):
        for t in np.random.permutation(T):
            e = deal[t]; j = e * C + place[e, fill[e]]; fill[e] += 1; slot_token[j] = t; pos[r, t] = j
    g = np.random.uniform(0.2, 0.8, T)
    return {
        "xT": (n((K, T)) * s).astype(np.float32),
        "w": (n((E, K, N)) / np.sqrt(K) / s[None]).astype(np.float32),
        "b": (0.3 * n((N, E))).astype(np.float32),
        "gate": np.stack([np.tile(g, (N, 1)), np.tile(1.0 - g, (N, 1))]).astype(np.float32),
        "offs": striped(slot_token),
        "pos1": striped(pos[0]),
        "pos2": striped(pos[1]),
    }


def reference(xT, w, b, gate, offs, pos1, pos2):
    idx = unstriped(offs)
    xq = mxq(f64(xT)[:, idx], 0, "e4m3")
    y = by_expert(mxq(f64(w), 1, "e4m3"), xq)
    y = y + np.repeat(f64(b), C, axis=1)
    return f64(gate[0]) * y[:, unstriped(pos1)] + f64(gate[1]) * y[:, unstriped(pos2)]

@@ -1,0 +1,142 @@
+from contextlib import ExitStack
+
+import concourse.mybir as mybir
+
+K, T, E, C, N = 1536, 512, 4, 256, 256
+FLOPS = 2 * E * C * K * N
+
+F32 = mybir.dt.float32
+BF16 = mybir.dt.bfloat16
+U32 = mybir.dt.uint32
+U16 = mybir.dt.uint16
+U8 = mybir.dt.uint8
+FP8X4 = mybir.dt.float8_e4m3fn_x4
+IDENTITY = mybir.ActivationFunctionType.Identity
+MULT = mybir.AluOpType.mult
+ADD = mybir.AluOpType.add
+
+P = 128
+PACK = 4
+K_PASS = P * PACK
+PASSES = K // K_PASS
+SLOTS = E * C
+HALVES = N // P
+
+CUTS = ((0, 384), (384, 384), (768, 256))
+X_PIECES = (((0, 256, 256), (256, 512, 160)), ((0, 512, 128),), ((0, 512, 128),))
+W_SHARES = {(2, 1): (256, 0), (3, 0): (256, 0), (3, 2): (128, 0)}
+W_SPLIT = ((3, 2),)
+BIAS_AFTER = (2, 2)
+
+
+def interleave(copy, out, rows, lo, hi):
+    if lo < hi:
+        copy(
+            out[:, lo:hi, :].rearrange("p (c i) t -> p c t i", i=4),
+            rows[:, :, lo:hi].rearrange("p t (c i) -> p c t i", i=4),
+        )
+
+
+def tile_routed_moe_kernel(tc, xT, w, b, gate, offs, pos1, pos2, out):
+    nc = tc.nc
+
+    def gpsimd_copy(dst, rows):
+        nc.gpsimd.tensor_scalar(dst, rows, 1.0, 0.0, op0=MULT, op1=ADD)
+
+    with ExitStack() as ctx:
+        keep = ctx.enter_context(tc.tile_pool(name="keep", bufs=1))
+        psum = ctx.enter_context(tc.psum_pool(name="psum", bufs=1))
+
+        offs_sb = keep.tile([P, SLOTS // 16], U16, name="offs_sb")
+        pos_sb = [keep.tile([P, T // 16], U16, name=f"pos_sb{r}") for r in range(2)]
+        b_sb = keep.tile([P, HALVES, E], F32, name="b_sb")
+        x_raw = [keep.tile([P, PACK, T], F32, name=f"x_raw{a}") for a in range(PASSES)]
+        x_grouped = [keep.tile([P, T, PACK], BF16, name=f"x_grouped{a}", align_bytes=64) for a in range(PASSES)]
+        x_codes = [keep.tile([P, T], U32, name=f"x_codes{a}", align_bytes=64) for a in range(PASSES)]
+        x_scales = keep.tile([P, T], U8, name="x_scales", align_bytes=64)
+        s_codes = [keep.tile([P, SLOTS], U32, name=f"s_codes{a}", align_bytes=64) for a in range(PASSES)]
+        s_scales = keep.tile([P, SLOTS], U8, name="s_scales", align_bytes=64)
+        gate_sb = [keep.tile([P, 2, T], F32, name=f"gate_sb{h}") for h in range(HALVES)]
+        y = [keep.tile([P, SLOTS], F32, name=f"y{h}") for h in range(HALVES)]
+
+        nc.gpsimd.memset(x_scales[:], 0)
+
+        for a in range(PASSES):
+            rows = xT[a * K_PASS : (a + 1) * K_PASS, :].rearrange("(p t) n -> p t n", t=PACK)
+            for lo, hi, v in X_PIECES[a]:
+                nc.sync.dma_start(out=x_raw[a][:, :, lo:hi], in_=rows[:, :, lo:hi])
+            if a == 0:
+                nc.sync.dma_start(out=offs_sb[:], in_=offs)
+
+        w_raw = {}
+        for e in range(E):
+            for a in range(PASSES):
+                w_raw[e, a] = keep.tile([P, PACK, N], F32, name=f"w_raw{e}_{a}")
+                rows = w[e, a * K_PASS : (a + 1) * K_PASS, :].rearrange("(p t) n -> p t n", t=PACK)
+                nc.sync.dma_start(out=w_raw[e, a][:], in_=rows)
+                if (e, a) == BIAS_AFTER:
+                    nc.sync.dma_start(out=b_sb[:], in_=b.rearrange("(h p) e -> p h e", p=P))
+        nc.sync.dma_start(out=pos_sb[0][:], in_=pos1)
+        nc.sync.dma_start(out=pos_sb[1][:], in_=pos2)
+        for h in range(HALVES):
+            nc.sync.dma_start(out=gate_sb[h][:], in_=gate[:, h * P : (h + 1) * P, :].rearrange("r p t -> p r t"))
+
+        for a in range(PASSES):
+            for lo, hi, v in X_PIECES[a]:
+                interleave(nc.vector.tensor_copy, x_grouped[a], x_raw[a], lo, lo + v)
+                interleave(nc.scalar.copy, x_grouped[a], x_raw[a], lo + v, hi)
+                nc.vector.quantize_mx(
+                    out=x_codes[a][:, lo:hi].bitcast(FP8X4),
+                    scales=x_scales[4 * a : P, lo:hi],
+                    in_=x_grouped[a][:, lo:hi, :].rearrange("p n t -> p (n t)"),
+                )
+            for lo, n in CUTS:
+                picked = offs_sb[:, lo // 16 : (lo + n) // 16]
+                nc.vector.tensor_copy(s_codes[a][:, lo : lo + n], x_codes[a][:].indirect(picked))
+        for lo, n in CUTS:
+            picked = offs_sb[:, lo // 16 : (lo + n) // 16]
+            nc.vector.tensor_copy(s_scales[:, lo : lo + n], x_scales[:].indirect(picked))
+
+        w_codes = {}
+        w_scales = {}
+        for e in range(E):
+            for a in range(PASSES):
+                w_grouped = keep.tile([P, N, PACK], BF16, name=f"w_grouped{e}_{a}", align_bytes=64)
+                w_codes[e, a] = keep.tile([P, N], U32, name=f"w_codes{e}_{a}", align_bytes=64)
+                w_scales[e, a] = keep.tile([P, N], U8, name=f"w_scales{e}_{a}", align_bytes=64)
+                v, g = W_SHARES.get((e, a), (0, 0))
+                interleave(nc.vector.tensor_copy, w_grouped, w_raw[e, a], 0, v)
+                interleave(gpsimd_copy, w_grouped, w_raw[e, a], v, v + g)
+                interleave(nc.scalar.copy, w_grouped, w_raw[e, a], v + g, N)
+                width = P if (e, a) in W_SPLIT else N
+                for lo in range(0, N, width):
+                    nc.vector.quantize_mx(
+                        out=w_codes[e, a][:, lo : lo + width].bitcast(FP8X4),
+                        scales=w_scales[e, a][:, lo : lo + width],
+                        in_=w_grouped[:, lo : lo + width, :].rearrange("p n t -> p (n t)"),
+                    )
+
+        for e in range(E):
+            slots = slice(e * C, (e + 1) * C)
+            for h in range(HALVES):
+                acc = psum.tile([P, C], F32, name=f"acc{e}_{h}")
+                features = slice(h * P, (h + 1) * P)
+                for a in range(PASSES):
+                    nc.tensor.matmul_mx(
+                        out=acc[:],
+                        lhsT=w_codes[e, a][:, features].bitcast(FP8X4),
+                        lhsT_scale=w_scales[e, a][:, features],
+                        rhs=s_codes[a][:, slots].bitcast(FP8X4),
+                        rhs_scale=s_scales[4 * a : P, slots],
+                        start=(a == 0),
+                        stop=(a == PASSES - 1),
+                    )
+                nc.scalar.activation(y[h][:, slots], acc[:], IDENTITY, bias=b_sb[:, h, e : e + 1])
+
+        for h in range(HALVES):
+            part = [keep.tile([P, T], F32, name=f"part{h}_{r}") for r in range(2)]
+            total = keep.tile([P, T], F32, name=f"total{h}")
+            for r in range(2):
+                nc.vector.tensor_tensor(part[r][:], y[h][:].indirect(pos_sb[r][:]), gate_sb[h][:, r, :], MULT)
+            nc.vector.tensor_tensor(total[:], part[0][:], part[1][:], ADD)
+            nc.sync.dma_start(out=out[h * P : (h + 1) * P, :], in_=total[:])

@@ -21,12 +21,15 @@ K_PASS = P * PACK
 PASSES = K // K_PASS
 SLOTS = E * C
 HALVES = N // P
+WINDOW = 1376
+I32 = mybir.dt.int32
 
-CUTS = ((0, 384), (384, 384), (768, 256))
-X_PIECES = (((0, 256, 256), (256, 512, 160)), ((0, 512, 128),), ((0, 512, 128),))
-W_SHARES = {(2, 1): (256, 0), (3, 0): (256, 0), (3, 2): (128, 0)}
+CUTS = ((0, 1024),)
+X_PIECES = (((0, 256, 128), (256, 512, 160)), ((0, 512, 128),), ((0, 512, 96),))
+W_SHARES = {(1, 0): (256, 0), (2, 0): (128, 0), (3, 0): (192, 0), (3, 2): (192, 0)}
 W_SPLIT = ((3, 2),)
-BIAS_AFTER = (2, 2)
+Y_VECTOR = ((3, 0),)
+BIAS_AFTER = (3, 1)
 
 
 def interleave(copy, out, rows, lo, hi):
@@ -40,9 +43,6 @@ def interleave(copy, out, rows, lo, hi):
 def tile_routed_moe_kernel(tc, xT, w, b, gate, offs, pos1, pos2, out):
     nc = tc.nc
 
-    def gpsimd_copy(dst, rows):
-        nc.gpsimd.tensor_scalar(dst, rows, 1.0, 0.0, op0=MULT, op1=ADD)
-
     with ExitStack() as ctx:
         keep = ctx.enter_context(tc.tile_pool(name="keep", bufs=1))
         psum = ctx.enter_context(tc.psum_pool(name="psum", bufs=1))
@@ -52,14 +52,16 @@ def tile_routed_moe_kernel(tc, xT, w, b, gate, offs, pos1, pos2, out):
         b_sb = keep.tile([P, HALVES, E], F32, name="b_sb")
         x_raw = [keep.tile([P, PACK, T], F32, name=f"x_raw{a}") for a in range(PASSES)]
         x_grouped = [keep.tile([P, T, PACK], BF16, name=f"x_grouped{a}", align_bytes=64) for a in range(PASSES)]
-        x_codes = [keep.tile([P, T], U32, name=f"x_codes{a}", align_bytes=64) for a in range(PASSES)]
-        x_scales = keep.tile([P, T], U8, name="x_scales", align_bytes=64)
+        x_codes = [keep.tile([P, WINDOW], I32, name=f"x_codes{a}", align_bytes=64) for a in range(PASSES)]
+        x_scales = keep.tile([P, WINDOW], U8, name="x_scales", align_bytes=64)
         s_codes = [keep.tile([P, SLOTS], U32, name=f"s_codes{a}", align_bytes=64) for a in range(PASSES)]
         s_scales = keep.tile([P, SLOTS], U8, name="s_scales", align_bytes=64)
         gate_sb = [keep.tile([P, 2, T], F32, name=f"gate_sb{h}") for h in range(HALVES)]
         y = [keep.tile([P, SLOTS], F32, name=f"y{h}") for h in range(HALVES)]
 
-        nc.gpsimd.memset(x_scales[:], 0)
+        nc.gpsimd.memset(x_scales[:].bitcast(I32), 0)
+        for a in range(PASSES):
+            nc.gpsimd.memset(x_codes[a][:, T:], 0)
 
         for a in range(PASSES):
             rows = xT[a * K_PASS : (a + 1) * K_PASS, :].rearrange("(p t) n -> p t n", t=PACK)
@@ -92,7 +94,7 @@ def tile_routed_moe_kernel(tc, xT, w, b, gate, offs, pos1, pos2, out):
                 )
             for lo, n in CUTS:
                 picked = offs_sb[:, lo // 16 : (lo + n) // 16]
-                nc.vector.tensor_copy(s_codes[a][:, lo : lo + n], x_codes[a][:].indirect(picked))
+                nc.vector.tensor_copy(s_codes[a][:, lo : lo + n], x_codes[a][:].bitcast(U32).indirect(picked))
         for lo, n in CUTS:
             picked = offs_sb[:, lo // 16 : (lo + n) // 16]
             nc.vector.tensor_copy(s_scales[:, lo : lo + n], x_scales[:].indirect(picked))
@@ -106,7 +108,6 @@ def tile_routed_moe_kernel(tc, xT, w, b, gate, offs, pos1, pos2, out):
                 w_scales[e, a] = keep.tile([P, N], U8, name=f"w_scales{e}_{a}", align_bytes=64)
                 v, g = W_SHARES.get((e, a), (0, 0))
                 interleave(nc.vector.tensor_copy, w_grouped, w_raw[e, a], 0, v)
-                interleave(gpsimd_copy, w_grouped, w_raw[e, a], v, v + g)
                 interleave(nc.scalar.copy, w_grouped, w_raw[e, a], v + g, N)
                 width = P if (e, a) in W_SPLIT else N
                 for lo in range(0, N, width):
@@ -116,9 +117,9 @@ def tile_routed_moe_kernel(tc, xT, w, b, gate, offs, pos1, pos2, out):
                         in_=w_grouped[:, lo : lo + width, :].rearrange("p n t -> p (n t)"),
                     )
 
-        for e in range(E):
-            slots = slice(e * C, (e + 1) * C)
-            for h in range(HALVES):
+        for h in range(HALVES):
+            for e in range(E):
+                slots = slice(e * C, (e + 1) * C)
                 acc = psum.tile([P, C], F32, name=f"acc{e}_{h}")
                 features = slice(h * P, (h + 1) * P)
                 for a in range(PASSES):
@@ -131,7 +132,10 @@ def tile_routed_moe_kernel(tc, xT, w, b, gate, offs, pos1, pos2, out):
                         start=(a == 0),
                         stop=(a == PASSES - 1),
                     )
-                nc.scalar.activation(y[h][:, slots], acc[:], IDENTITY, bias=b_sb[:, h, e : e + 1])
+                if (e, h) in Y_VECTOR:
+                    nc.vector.tensor_scalar_add(y[h][:, slots], acc[:], b_sb[:, h, e : e + 1])
+                else:
+                    nc.scalar.activation(y[h][:, slots], acc[:], IDENTITY, bias=b_sb[:, h, e : e + 1])
 
         for h in range(HALVES):
             part = [keep.tile([P, T], F32, name=f"part{h}_{r}") for r in range(2)]

from contextlib import ExitStack

import concourse.mybir as mybir

K, T, E, C, N = 1536, 512, 4, 256, 256
FLOPS = 2 * E * C * K * N

F32 = mybir.dt.float32
BF16 = mybir.dt.bfloat16
U32 = mybir.dt.uint32
U16 = mybir.dt.uint16
U8 = mybir.dt.uint8
FP8X4 = mybir.dt.float8_e4m3fn_x4
IDENTITY = mybir.ActivationFunctionType.Identity
MULT = mybir.AluOpType.mult
ADD = mybir.AluOpType.add

P = 128
PACK = 4
K_PASS = P * PACK
PASSES = K // K_PASS
SLOTS = E * C
HALVES = N // P
WINDOW = 1376
I32 = mybir.dt.int32

CUTS = ((0, 1024),)
X_PIECES = (((0, 256, 128), (256, 512, 160)), ((0, 512, 128),), ((0, 512, 96),))
W_SHARES = {(1, 0): (256, 0), (2, 0): (128, 0), (3, 0): (192, 0), (3, 2): (192, 0)}
W_SPLIT = ((3, 2),)
Y_VECTOR = ((3, 0),)
BIAS_AFTER = (3, 1)


def interleave(copy, out, rows, lo, hi):
    if lo < hi:
        copy(
            out[:, lo:hi, :].rearrange("p (c i) t -> p c t i", i=4),
            rows[:, :, lo:hi].rearrange("p t (c i) -> p c t i", i=4),
        )


def tile_routed_moe_kernel(tc, xT, w, b, gate, offs, pos1, pos2, out):
    nc = tc.nc

    with ExitStack() as ctx:
        keep = ctx.enter_context(tc.tile_pool(name="keep", bufs=1))
        psum = ctx.enter_context(tc.psum_pool(name="psum", bufs=1))

        offs_sb = keep.tile([P, SLOTS // 16], U16, name="offs_sb")
        pos_sb = [keep.tile([P, T // 16], U16, name=f"pos_sb{r}") for r in range(2)]
        b_sb = keep.tile([P, HALVES, E], F32, name="b_sb")
        x_raw = [keep.tile([P, PACK, T], F32, name=f"x_raw{a}") for a in range(PASSES)]
        x_grouped = [keep.tile([P, T, PACK], BF16, name=f"x_grouped{a}", align_bytes=64) for a in range(PASSES)]
        x_codes = [keep.tile([P, WINDOW], I32, name=f"x_codes{a}", align_bytes=64) for a in range(PASSES)]
        x_scales = keep.tile([P, WINDOW], U8, name="x_scales", align_bytes=64)
        s_codes = [keep.tile([P, SLOTS], U32, name=f"s_codes{a}", align_bytes=64) for a in range(PASSES)]
        s_scales = keep.tile([P, SLOTS], U8, name="s_scales", align_bytes=64)
        gate_sb = [keep.tile([P, 2, T], F32, name=f"gate_sb{h}") for h in range(HALVES)]
        y = [keep.tile([P, SLOTS], F32, name=f"y{h}") for h in range(HALVES)]

        nc.gpsimd.memset(x_scales[:].bitcast(I32), 0)
        for a in range(PASSES):
            nc.gpsimd.memset(x_codes[a][:, T:], 0)

        for a in range(PASSES):
            rows = xT[a * K_PASS : (a + 1) * K_PASS, :].rearrange("(p t) n -> p t n", t=PACK)
            for lo, hi, v in X_PIECES[a]:
                nc.sync.dma_start(out=x_raw[a][:, :, lo:hi], in_=rows[:, :, lo:hi])
            if a == 0:
                nc.sync.dma_start(out=offs_sb[:], in_=offs)

        w_raw = {}
        for e in range(E):
            for a in range(PASSES):
                w_raw[e, a] = keep.tile([P, PACK, N], F32, name=f"w_raw{e}_{a}")
                rows = w[e, a * K_PASS : (a + 1) * K_PASS, :].rearrange("(p t) n -> p t n", t=PACK)
                nc.sync.dma_start(out=w_raw[e, a][:], in_=rows)
                if (e, a) == BIAS_AFTER:
                    nc.sync.dma_start(out=b_sb[:], in_=b.rearrange("(h p) e -> p h e", p=P))
        nc.sync.dma_start(out=pos_sb[0][:], in_=pos1)
        nc.sync.dma_start(out=pos_sb[1][:], in_=pos2)
        for h in range(HALVES):
            nc.sync.dma_start(out=gate_sb[h][:], in_=gate[:, h * P : (h + 1) * P, :].rearrange("r p t -> p r t"))

        for a in range(PASSES):
            for lo, hi, v in X_PIECES[a]:
                interleave(nc.vector.tensor_copy, x_grouped[a], x_raw[a], lo, lo + v)
                interleave(nc.scalar.copy, x_grouped[a], x_raw[a], lo + v, hi)
                nc.vector.quantize_mx(
                    out=x_codes[a][:, lo:hi].bitcast(FP8X4),
                    scales=x_scales[4 * a : P, lo:hi],
                    in_=x_grouped[a][:, lo:hi, :].rearrange("p n t -> p (n t)"),
                )
            for lo, n in CUTS:
                picked = offs_sb[:, lo // 16 : (lo + n) // 16]
                nc.vector.tensor_copy(s_codes[a][:, lo : lo + n], x_codes[a][:].bitcast(U32).indirect(picked))
        for lo, n in CUTS:
            picked = offs_sb[:, lo // 16 : (lo + n) // 16]
            nc.vector.tensor_copy(s_scales[:, lo : lo + n], x_scales[:].indirect(picked))

        w_codes = {}
        w_scales = {}
        for e in range(E):
            for a in range(PASSES):
                w_grouped = keep.tile([P, N, PACK], BF16, name=f"w_grouped{e}_{a}", align_bytes=64)
                w_codes[e, a] = keep.tile([P, N], U32, name=f"w_codes{e}_{a}", align_bytes=64)
                w_scales[e, a] = keep.tile([P, N], U8, name=f"w_scales{e}_{a}", align_bytes=64)
                v, g = W_SHARES.get((e, a), (0, 0))
                interleave(nc.vector.tensor_copy, w_grouped, w_raw[e, a], 0, v)
                interleave(nc.scalar.copy, w_grouped, w_raw[e, a], v + g, N)
                width = P if (e, a) in W_SPLIT else N
                for lo in range(0, N, width):
                    nc.vector.quantize_mx(
                        out=w_codes[e, a][:, lo : lo + width].bitcast(FP8X4),
                        scales=w_scales[e, a][:, lo : lo + width],
                        in_=w_grouped[:, lo : lo + width, :].rearrange("p n t -> p (n t)"),
                    )

        for h in range(HALVES):
            for e in range(E):
                slots = slice(e * C, (e + 1) * C)
                acc = psum.tile([P, C], F32, name=f"acc{e}_{h}")
                features = slice(h * P, (h + 1) * P)
                for a in range(PASSES):
                    nc.tensor.matmul_mx(
                        out=acc[:],
                        lhsT=w_codes[e, a][:, features].bitcast(FP8X4),
                        lhsT_scale=w_scales[e, a][:, features],
                        rhs=s_codes[a][:, slots].bitcast(FP8X4),
                        rhs_scale=s_scales[4 * a : P, slots],
                        start=(a == 0),
                        stop=(a == PASSES - 1),
                    )
                if (e, h) in Y_VECTOR:
                    nc.vector.tensor_scalar_add(y[h][:, slots], acc[:], b_sb[:, h, e : e + 1])
                else:
                    nc.scalar.activation(y[h][:, slots], acc[:], IDENTITY, bias=b_sb[:, h, e : e + 1])

        for h in range(HALVES):
            part = [keep.tile([P, T], F32, name=f"part{h}_{r}") for r in range(2)]
            total = keep.tile([P, T], F32, name=f"total{h}")
            for r in range(2):
                nc.vector.tensor_tensor(part[r][:], y[h][:].indirect(pos_sb[r][:]), gate_sb[h][:, r, :], MULT)
            nc.vector.tensor_tensor(total[:], part[0][:], part[1][:], ADD)
            nc.sync.dma_start(out=out[h * P : (h + 1) * P, :], in_=total[:])
